import numpy as np
import ml_dtypes


def mxq(x, axis, fmt="e4m3"):
    dtype, down = {"e4m3": (ml_dtypes.float8_e4m3fn, 7), "e5m2": (ml_dtypes.float8_e5m2, 14)}[fmt]
    v = np.moveaxis(np.asarray(x, np.float32).astype(ml_dtypes.bfloat16).astype(np.float64), axis, -1)
    blocks = v.reshape(v.shape[:-1] + (-1, 32))
    amax = np.abs(blocks).max(-1, keepdims=True)
    byte = np.maximum(np.where(amax > 0, np.frexp(amax)[1] - 1 + 127, 0) - down, 1)
    scale = np.exp2(byte - 127.0)
    codes = (blocks / scale).astype(np.float32).astype(dtype).astype(np.float64)
    return np.moveaxis((codes * scale).reshape(v.shape), -1, axis)


WIDE = False


def mx_kscale(k):
    if not WIDE:
        return np.ones(k)
    levels = np.array([10, -10, 5, -5, 0])
    if k % 512:
        return np.exp2(np.random.permutation(np.resize(levels, k // 32))).repeat(32)
    a = np.empty((k // 512, 16))
    for p in range(k // 512):
        a[p, :8] = np.random.permutation(np.resize(levels, 8))
        for g in range(8):
            far = levels[np.abs(levels - a[p, g]) >= 10]
            a[p, g + 8] = far[np.random.randint(len(far))]
    return np.exp2(a.ravel()).repeat(32)


def f64(x):
    return np.asarray(x).astype(np.float64)


def striped(idx):
    return np.tile(idx.reshape(-1, 16).T, (8, 1)).astype(np.uint16)


def unstriped(offs):
    return offs[:16].T.reshape(-1).astype(np.int64)


def pack_weight(w):
    k, n = w.shape
    w = f64(np.asarray(w, np.float32).astype(ml_dtypes.bfloat16)).reshape(k // 32, 32, n)
    amax = np.abs(w).max(1)
    byte = np.clip(np.where(amax > 0, np.frexp(amax)[1] - 1 + 127 - 7, 1), 1, 254)
    scaled = (w * np.exp2(127.0 - byte)[:, None, :]).reshape(k, n).astype(np.float32)
    words = np.ascontiguousarray(scaled.reshape(k // 512, 128, 4, n).transpose(0, 1, 3, 2)).astype(ml_dtypes.float8_e4m3fn).view(np.uint8)
    return words, np.ascontiguousarray(byte.astype(np.uint8).reshape(k // 512, 16, n))


def unpack_weight(words, scales):
    g, p, n, _ = words.shape
    vals = np.ascontiguousarray(words).view(ml_dtypes.float8_e4m3fn).astype(np.float64) * np.repeat(np.exp2(scales.astype(np.float64) - 127.0), 8, axis=1)[..., None]
    return vals.transpose(0, 1, 3, 2).reshape(g * 512, n)


def relu(v):
    return np.maximum(v, 0.0)


K, T, S, V, R = 1024, 2048, 512, 256, 128


def setup_inputs():
    n = np.random.standard_normal
    s = mx_kscale(K)[:, None]
    c = mx_kscale(S)
    packed_xT = pack_weight(n((K, T)) * s)
    return {
        "x_words": packed_xT[0],
        "x_scales": packed_xT[1],
        "rew": (n((K, V)) / np.sqrt(K) / s).astype(np.float32),
        "pert": (n((S, R)) / np.sqrt(S) / c[:, None]).astype(np.float32),
        "base": (0.5 * n((S, 1))).astype(np.float32),
        "isig": (np.random.uniform(0.6, 1.4, (S, 1)) * c[:, None]).astype(np.float32),
        "theta": (n((R, V))).astype(np.float32),
        "offs": striped(np.random.permutation(T)[:S]),
    }


def reference(x_words, x_scales, rew, pert, base, isig, theta, offs):
    xq = unpack_weight(x_words, x_scales)[:, unstriped(offs)]
    rewq = mxq(f64(rew), 0, "e4m3")
    y = xq.T @ rewq
    util = relu(y + f64(base)) - (0.4 * (relu(-1.0 * (y + f64(base)) - 0.5)))
    wu = f64(isig) * util
    grad = mxq(f64(pert), 0, "e4m3").T @ mxq(wu, 0, "e4m3")
    g2 = (grad) ** 2
    gm = g2.mean(axis=1, keepdims=True)
    return f64(theta) + grad / np.sqrt(gm + 0.1)

@@ -1,0 +1,170 @@
+from contextlib import ExitStack
+
+import concourse.mybir as mybir
+
+F32 = mybir.dt.float32
+BF16 = mybir.dt.bfloat16
+I32 = mybir.dt.int32
+U32 = mybir.dt.uint32
+U16 = mybir.dt.uint16
+U8 = mybir.dt.uint8
+FP8X4 = mybir.dt.float8_e4m3fn_x4
+ALU = mybir.AluOpType
+ACT = mybir.ActivationFunctionType
+
+P = 128
+PACK = 4
+K, T, S, V, R = 1024, 2048, 512, 256, 128
+PASSES = K // (P * PACK)
+HALF = V // 2
+FLOPS = 2 * K * S * V + 2 * S * R * V
+
+
+def tile_picked_yevos_norm_p_kernel(tc, x_words, x_scales, rew, pert, base, isig, theta, offs, out):
+    nc = tc.nc
+    with ExitStack() as ctx:
+        keep = ctx.enter_context(tc.tile_pool(name="keep", bufs=1))
+        psum = ctx.enter_context(tc.psum_pool(name="psum", bufs=1))
+
+        def sbuf(name, shape, dtype, tag=None):
+            return keep.tile(shape, dtype, name=name, tag=tag or name, align_bytes=64)
+
+        def quantize(name, grouped, width, tag=None):
+            codes = sbuf(name + "_codes", [P, width], U32, tag)
+            scales = sbuf(name + "_scales", [P, width], U8)
+            nc.vector.quantize_mx(out=codes[:].bitcast(FP8X4), scales=scales[:], in_=grouped.rearrange("p c j -> p (c j)"))
+            return codes, scales
+
+        word_table = [sbuf("word_table%d" % g, [P, T], U32) for g in range(PASSES)]
+        rew_raw = [sbuf("rew_raw%d" % g, [P, PACK, V], F32) for g in range(PASSES)]
+
+        def load_words(g):
+            nc.sync.dma_start(
+                out=word_table[g][:].bitcast(I32),
+                in_=x_words[g].rearrange("p n t -> p (n t)").bitcast(I32),
+            )
+
+        def load_rew(g):
+            nc.sync.dma_start(
+                out=rew_raw[g][:],
+                in_=rew[g * P * PACK : (g + 1) * P * PACK, :].rearrange("(p j) v -> p j v", j=PACK),
+            )
+
+        offsets = keep.tile([P, S // 16], U16, name="offsets")
+        load_words(0)
+        nc.sync.dma_start(offsets[:], offs)
+        load_rew(0)
+        load_rew(1)
+        load_words(1)
+        pert_raw = sbuf("pert_raw", [P, PACK, R], F32)
+        nc.sync.dma_start(out=pert_raw[:], in_=pert.rearrange("(p j) r -> p j r", j=PACK))
+        theta_sb = sbuf("theta_sb", [P, V], F32)
+        nc.sync.dma_start(out=theta_sb[:], in_=theta)
+
+        scale_table = sbuf("scale_table", [P, T], U8)
+        nc.vector.memset(scale_table[:].bitcast(I32), 0)
+        for q in range(4):
+            nc.gpsimd.dma_start(
+                out=scale_table[32 * q : 32 * q + 4 * PASSES, :].bitcast(I32),
+                in_=x_scales[:, 4 * q : 4 * q + 4, :].bitcast(I32),
+            )
+
+        base_sb = sbuf("base_sb", [P, PACK], F32)
+        isig_sb = sbuf("isig_sb", [P, PACK], F32)
+        nc.scalar.dma_start(out=base_sb[:], in_=base.rearrange("(p j) o -> p (j o)", j=PACK))
+        nc.scalar.dma_start(out=isig_sb[:], in_=isig.rearrange("(p j) o -> p (j o)", j=PACK))
+
+        picked_words = []
+
+        def gather_words(g, tag):
+            picked = sbuf("picked_words%d" % g, [P, PACK, P], U32, tag)
+            nc.vector.tensor_copy(picked[:].rearrange("p j m -> p m j"), word_table[g][:].indirect(offsets[:]))
+            picked_words.append(picked)
+
+        gather_words(0, None)
+        picked_scales = sbuf("picked_scales", [P, S], U8)
+        nc.vector.tensor_copy(picked_scales[:], scale_table[:].indirect(offsets[:]))
+        dealt_scales = sbuf("dealt_scales", [P, PACK, P], U8)
+        nc.vector.tensor_copy(dealt_scales[:], picked_scales[:].rearrange("p (m j) -> p j m", j=PACK))
+
+        rew_mx = []
+        for g, tag in enumerate(("scale_table", "picked_scales")):
+            grouped = sbuf("rew_grouped%d" % g, [P, V, PACK], BF16)
+            nc.scalar.activation(grouped[:], rew_raw[g][:].rearrange("p j v -> p v j"), ACT.Copy, scale=-1.0)
+            rew_mx.append(quantize("rew%d" % g, grouped[:], V, tag))
+        gather_words(1, "rew_grouped1")
+
+        knee = sbuf("knee", [P, PACK], F32)
+        neg_isig = sbuf("neg_isig", [P, PACK], F32)
+        nc.scalar.activation(knee[:], base_sb[:], ACT.Copy, scale=-0.4, bias=-0.2)
+        nc.scalar.activation(neg_isig[:], isig_sb[:], ACT.Copy, scale=-1.0)
+
+        pert_grouped = sbuf("pert_grouped", [P, R, PACK], BF16)
+        nc.scalar.activation(pert_grouped[:], pert_raw[:].rearrange("p j r -> p r j"), ACT.Copy)
+        pert_codes, pert_scales = quantize("pert", pert_grouped[:], R, "word_table1")
+
+        neg_y = [psum.tile([P, V], F32, name="neg_y%d" % j) for j in range(PACK)]
+        for g in range(PASSES):
+            rew_codes, rew_scales = rew_mx[g]
+            for j in range(PACK):
+                nc.tensor.matmul_mx(
+                    out=neg_y[j][:],
+                    lhsT=picked_words[g][:, j, :].bitcast(FP8X4),
+                    lhsT_scale=dealt_scales[4 * g :, j, :],
+                    rhs=rew_codes[:].bitcast(FP8X4),
+                    rhs_scale=rew_scales[:],
+                    start=(g == 0),
+                    stop=(g == PASSES - 1),
+                )
+
+        halves = [slice(h * HALF, (h + 1) * HALF) for h in range(2)]
+        neg_util = sbuf("neg_util", [P, PACK, V], F32)
+        for j in range(PACK):
+            penalty = sbuf("penalty%d" % j, [P, V], F32)
+            nc.scalar.activation(penalty[:], neg_y[j][:], ACT.Relu, scale=0.4, bias=knee[:, j : j + 1])
+            for cols in halves if j == PACK - 1 else [slice(0, V)]:
+                nc.vector.scalar_tensor_tensor(
+                    out=neg_util[:, j, cols],
+                    in0=neg_y[j][:, cols],
+                    scalar=base_sb[:, j : j + 1],
+                    in1=penalty[:, cols],
+                    op0=ALU.subtract,
+                    op1=ALU.min,
+                )
+
+        wu = [sbuf("wu%d" % h, [P, HALF, PACK], BF16) for h in range(2)]
+        for h, cols in enumerate(halves):
+            nc.vector.tensor_tensor(
+                out=wu[h][:],
+                in0=neg_util[:, :, cols].rearrange("p j v -> p v j"),
+                in1=neg_isig[:].unsqueeze(1).to_broadcast([P, HALF, PACK]),
+                op=ALU.mult,
+            )
+
+        grad = [psum.tile([P, HALF], F32, name="grad%d" % h) for h in range(2)]
+        square_sum = [sbuf("square_sum%d" % h, [P, 1], F32) for h in range(2)]
+        first_part = sbuf("first_part", [P, 1], F32)
+        for h in range(2):
+            wu_codes, wu_scales = quantize("wu%d" % h, wu[h][:], HALF)
+            nc.tensor.matmul_mx(
+                out=grad[h][:],
+                lhsT=pert_codes[:].bitcast(FP8X4),
+                lhsT_scale=pert_scales[:],
+                rhs=wu_codes[:].bitcast(FP8X4),
+                rhs_scale=wu_scales[:],
+                start=True,
+                stop=True,
+            )
+            squares = sbuf("squares%d" % h, [P, HALF], F32)
+            nc.scalar.activation(squares[:], grad[h][:], ACT.Square, accum_out=square_sum[h][:])
+            if h == 0:
+                nc.scalar.activation(first_part[:], square_sum[0][:], ACT.Copy, scale=1.0 / V, bias=0.1)
+
+        inv_rms = sbuf("inv_rms", [P, 1], F32)
+        nc.scalar.activation(inv_rms[:], square_sum[1][:], ACT.Abs_reciprocal_sqrt, scale=1.0 / V, bias=first_part[:])
+        for h, (cols, queue) in enumerate(zip(halves, (nc.sync, nc.scalar))):
+            result = sbuf("result%d" % h, [P, HALF], F32)
+            nc.vector.scalar_tensor_tensor(
+                out=result[:], in0=grad[h][:], scalar=inv_rms[:], in1=theta_sb[:, cols], op0=ALU.mult, op1=ALU.add
+            )
+            queue.dma_start(out=out[:, cols], in_=result[:])

@@ -50,29 +50,34 @@ def tile_picked_yevos_norm_p_kernel(tc, x_words, x_scales, rew, pert, base, isig
                 in_=rew[g * P * PACK : (g + 1) * P * PACK, :].rearrange("(p j) v -> p j v", j=PACK),
             )
 
+        scale_table = sbuf("scale_table", [P, T], U8)
+        nc.gpsimd.memset(scale_table[:].bitcast(I32), 0)
         offsets = keep.tile([P, S // 16], U16, name="offsets")
         load_words(0)
         nc.sync.dma_start(offsets[:], offs)
+        for q in range(4):
+            nc.sync.dma_start(
+                out=scale_table[32 * q : 32 * q + 4 * PASSES, :].bitcast(I32),
+                in_=x_scales[:, 4 * q : 4 * q + 4, :].bitcast(I32),
+            )
+
         load_rew(0)
         load_rew(1)
         load_words(1)
+        base_sb = sbuf("base_sb", [P, PACK], F32)
+        isig_sb = sbuf("isig_sb", [P, PACK], F32)
+        nc.sync.dma_start(out=base_sb[:], in_=base.rearrange("(p j) o -> p (j o)", j=PACK))
+        nc.sync.dma_start(out=isig_sb[:], in_=isig.rearrange("(p j) o -> p (j o)", j=PACK))
         pert_raw = sbuf("pert_raw", [P, PACK, R], F32)
         nc.sync.dma_start(out=pert_raw[:], in_=pert.rearrange("(p j) r -> p j r", j=PACK))
         theta_sb = sbuf("theta_sb", [P, V], F32)
         nc.sync.dma_start(out=theta_sb[:], in_=theta)
 
-        scale_table = sbuf("scale_table", [P, T], U8)
-        nc.vector.memset(scale_table[:].bitcast(I32), 0)
-        for q in range(4):
-            nc.gpsimd.dma_start(
-                out=scale_table[32 * q : 32 * q + 4 * PASSES, :].bitcast(I32),
-                in_=x_scales[:, 4 * q : 4 * q + 4, :].bitcast(I32),
-            )
 
-        base_sb = sbuf("base_sb", [P, PACK], F32)
-        isig_sb = sbuf("isig_sb", [P, PACK], F32)
-        nc.scalar.dma_start(out=base_sb[:], in_=base.rearrange("(p j) o -> p (j o)", j=PACK))
-        nc.scalar.dma_start(out=isig_sb[:], in_=isig.rearrange("(p j) o -> p (j o)", j=PACK))
+        one = sbuf("one", [P, 1], F32)
+        warm = sbuf("warm", [P, 1], F32)
+        nc.vector.memset(one[:], 1.0)
+        nc.scalar.activation(warm[:], one[:], ACT.Abs_reciprocal_sqrt)
 
         picked_words = []
 

@@ -51,18 +51,18 @@ def tile_picked_yevos_norm_p_kernel(tc, x_words, x_scales, rew, pert, base, isig
             )
 
         scale_table = sbuf("scale_table", [P, T], U8)
-        nc.gpsimd.memset(scale_table[:].bitcast(I32), 0)
+        nc.vector.memset(scale_table[:].bitcast(I32), 0)
         offsets = keep.tile([P, S // 16], U16, name="offsets")
-        load_words(0)
+        load_rew(0)
         nc.sync.dma_start(offsets[:], offs)
-        for q in range(4):
-            nc.sync.dma_start(
+        for q, queue in enumerate((nc.sync, nc.sync, nc.sync, nc.sync)):
+            queue.dma_start(
                 out=scale_table[32 * q : 32 * q + 4 * PASSES, :].bitcast(I32),
                 in_=x_scales[:, 4 * q : 4 * q + 4, :].bitcast(I32),
             )
 
-        load_rew(0)
         load_rew(1)
+        load_words(0)
         load_words(1)
         base_sb = sbuf("base_sb", [P, PACK], F32)
         isig_sb = sbuf("isig_sb", [P, PACK], F32)
@@ -86,18 +86,18 @@ def tile_picked_yevos_norm_p_kernel(tc, x_words, x_scales, rew, pert, base, isig
             nc.vector.tensor_copy(picked[:].rearrange("p j m -> p m j"), word_table[g][:].indirect(offsets[:]))
             picked_words.append(picked)
 
-        gather_words(0, None)
         picked_scales = sbuf("picked_scales", [P, S], U8)
         nc.vector.tensor_copy(picked_scales[:], scale_table[:].indirect(offsets[:]))
         dealt_scales = sbuf("dealt_scales", [P, PACK, P], U8)
         nc.vector.tensor_copy(dealt_scales[:], picked_scales[:].rearrange("p (m j) -> p j m", j=PACK))
 
         rew_mx = []
-        for g, tag in enumerate(("scale_table", "picked_scales")):
+        for g in range(PASSES):
             grouped = sbuf("rew_grouped%d" % g, [P, V, PACK], BF16)
             nc.scalar.activation(grouped[:], rew_raw[g][:].rearrange("p j v -> p v j"), ACT.Copy, scale=-1.0)
-            rew_mx.append(quantize("rew%d" % g, grouped[:], V, tag))
-        gather_words(1, "rew_grouped1")
+            rew_mx.append(quantize("rew%d" % g, grouped[:], V))
+        gather_words(0, None)
+        gather_words(1, None)
 
         knee = sbuf("knee", [P, PACK], F32)
         neg_isig = sbuf("neg_isig", [P, PACK], F32)
@@ -106,7 +106,7 @@ def tile_picked_yevos_norm_p_kernel(tc, x_words, x_scales, rew, pert, base, isig
 
         pert_grouped = sbuf("pert_grouped", [P, R, PACK], BF16)
         nc.scalar.activation(pert_grouped[:], pert_raw[:].rearrange("p j r -> p r j"), ACT.Copy)
-        pert_codes, pert_scales = quantize("pert", pert_grouped[:], R, "word_table1")
+        pert_codes, pert_scales = quantize("pert", pert_grouped[:], R)
 
         neg_y = [psum.tile([P, V], F32, name="neg_y%d" % j) for j in range(PACK)]
         for g in range(PASSES):
@@ -137,14 +137,20 @@ def tile_picked_yevos_norm_p_kernel(tc, x_words, x_scales, rew, pert, base, isig
                     op1=ALU.min,
                 )
 
+        wu_rows = sbuf("wu_rows", [P, PACK, V], BF16)
+        for j in range(2):
+            nc.scalar.activation(wu_rows[:, j, :], neg_util[:, j, :], ACT.Copy, scale=neg_isig[:, j : j + 1])
+        for j, cols in ((2, slice(0, V)), (3, halves[0]), (3, halves[1])):
+            nc.vector.tensor_scalar(
+                out=wu_rows[:, j, cols],
+                in0=neg_util[:, j, cols],
+                scalar1=neg_isig[:, j : j + 1],
+                scalar2=None,
+                op0=ALU.mult,
+            )
         wu = [sbuf("wu%d" % h, [P, HALF, PACK], BF16) for h in range(2)]
         for h, cols in enumerate(halves):
-            nc.vector.tensor_tensor(
-                out=wu[h][:],
-                in0=neg_util[:, :, cols].rearrange("p j v -> p v j"),
-                in1=neg_isig[:].unsqueeze(1).to_broadcast([P, HALF, PACK]),
-                op=ALU.mult,
-            )
+            nc.vector.tensor_copy(wu[h][:], wu_rows[:, :, cols].rearrange("p j v -> p v j"))
 
         grad = [psum.tile([P, HALF], F32, name="grad%d" % h) for h in range(2)]
         square_sum = [sbuf("square_sum%d" % h, [P, 1], F32) for h in range(2)]

from contextlib import ExitStack

import concourse.mybir as mybir

F32 = mybir.dt.float32
BF16 = mybir.dt.bfloat16
I32 = mybir.dt.int32
U32 = mybir.dt.uint32
U16 = mybir.dt.uint16
U8 = mybir.dt.uint8
FP8X4 = mybir.dt.float8_e4m3fn_x4
ALU = mybir.AluOpType
ACT = mybir.ActivationFunctionType

P = 128
PACK = 4
K, T, S, V, R = 1024, 2048, 512, 256, 128
PASSES = K // (P * PACK)
HALF = V // 2
FLOPS = 2 * K * S * V + 2 * S * R * V


def tile_picked_yevos_norm_p_kernel(tc, x_words, x_scales, rew, pert, base, isig, theta, offs, out):
    nc = tc.nc
    with ExitStack() as ctx:
        keep = ctx.enter_context(tc.tile_pool(name="keep", bufs=1))
        psum = ctx.enter_context(tc.psum_pool(name="psum", bufs=1))

        def sbuf(name, shape, dtype, tag=None):
            return keep.tile(shape, dtype, name=name, tag=tag or name, align_bytes=64)

        def quantize(name, grouped, width, tag=None):
            codes = sbuf(name + "_codes", [P, width], U32, tag)
            scales = sbuf(name + "_scales", [P, width], U8)
            nc.vector.quantize_mx(out=codes[:].bitcast(FP8X4), scales=scales[:], in_=grouped.rearrange("p c j -> p (c j)"))
            return codes, scales

        word_table = [sbuf("word_table%d" % g, [P, T], U32) for g in range(PASSES)]
        rew_raw = [sbuf("rew_raw%d" % g, [P, PACK, V], F32) for g in range(PASSES)]

        def load_words(g):
            nc.sync.dma_start(
                out=word_table[g][:].bitcast(I32),
                in_=x_words[g].rearrange("p n t -> p (n t)").bitcast(I32),
            )

        def load_rew(g):
            nc.sync.dma_start(
                out=rew_raw[g][:],
                in_=rew[g * P * PACK : (g + 1) * P * PACK, :].rearrange("(p j) v -> p j v", j=PACK),
            )

        scale_table = sbuf("scale_table", [P, T], U8)
        nc.vector.memset(scale_table[:].bitcast(I32), 0)
        offsets = keep.tile([P, S // 16], U16, name="offsets")
        load_rew(0)
        nc.sync.dma_start(offsets[:], offs)
        for q, queue in enumerate((nc.sync, nc.sync, nc.sync, nc.sync)):
            queue.dma_start(
                out=scale_table[32 * q : 32 * q + 4 * PASSES, :].bitcast(I32),
                in_=x_scales[:, 4 * q : 4 * q + 4, :].bitcast(I32),
            )

        load_rew(1)
        load_words(0)
        load_words(1)
        base_sb = sbuf("base_sb", [P, PACK], F32)
        isig_sb = sbuf("isig_sb", [P, PACK], F32)
        nc.sync.dma_start(out=base_sb[:], in_=base.rearrange("(p j) o -> p (j o)", j=PACK))
        nc.sync.dma_start(out=isig_sb[:], in_=isig.rearrange("(p j) o -> p (j o)", j=PACK))
        pert_raw = sbuf("pert_raw", [P, PACK, R], F32)
        nc.sync.dma_start(out=pert_raw[:], in_=pert.rearrange("(p j) r -> p j r", j=PACK))
        theta_sb = sbuf("theta_sb", [P, V], F32)
        nc.sync.dma_start(out=theta_sb[:], in_=theta)


        one = sbuf("one", [P, 1], F32)
        warm = sbuf("warm", [P, 1], F32)
        nc.vector.memset(one[:], 1.0)
        nc.scalar.activation(warm[:], one[:], ACT.Abs_reciprocal_sqrt)

        picked_words = []

        def gather_words(g, tag):
            picked = sbuf("picked_words%d" % g, [P, PACK, P], U32, tag)
            nc.vector.tensor_copy(picked[:].rearrange("p j m -> p m j"), word_table[g][:].indirect(offsets[:]))
            picked_words.append(picked)

        picked_scales = sbuf("picked_scales", [P, S], U8)
        nc.vector.tensor_copy(picked_scales[:], scale_table[:].indirect(offsets[:]))
        dealt_scales = sbuf("dealt_scales", [P, PACK, P], U8)
        nc.vector.tensor_copy(dealt_scales[:], picked_scales[:].rearrange("p (m j) -> p j m", j=PACK))

        rew_mx = []
        for g in range(PASSES):
            grouped = sbuf("rew_grouped%d" % g, [P, V, PACK], BF16)
            nc.scalar.activation(grouped[:], rew_raw[g][:].rearrange("p j v -> p v j"), ACT.Copy, scale=-1.0)
            rew_mx.append(quantize("rew%d" % g, grouped[:], V))
        gather_words(0, None)
        gather_words(1, None)

        knee = sbuf("knee", [P, PACK], F32)
        neg_isig = sbuf("neg_isig", [P, PACK], F32)
        nc.scalar.activation(knee[:], base_sb[:], ACT.Copy, scale=-0.4, bias=-0.2)
        nc.scalar.activation(neg_isig[:], isig_sb[:], ACT.Copy, scale=-1.0)

        pert_grouped = sbuf("pert_grouped", [P, R, PACK], BF16)
        nc.scalar.activation(pert_grouped[:], pert_raw[:].rearrange("p j r -> p r j"), ACT.Copy)
        pert_codes, pert_scales = quantize("pert", pert_grouped[:], R)

        neg_y = [psum.tile([P, V], F32, name="neg_y%d" % j) for j in range(PACK)]
        for g in range(PASSES):
            rew_codes, rew_scales = rew_mx[g]
            for j in range(PACK):
                nc.tensor.matmul_mx(
                    out=neg_y[j][:],
                    lhsT=picked_words[g][:, j, :].bitcast(FP8X4),
                    lhsT_scale=dealt_scales[4 * g :, j, :],
                    rhs=rew_codes[:].bitcast(FP8X4),
                    rhs_scale=rew_scales[:],
                    start=(g == 0),
                    stop=(g == PASSES - 1),
                )

        halves = [slice(h * HALF, (h + 1) * HALF) for h in range(2)]
        neg_util = sbuf("neg_util", [P, PACK, V], F32)
        for j in range(PACK):
            penalty = sbuf("penalty%d" % j, [P, V], F32)
            nc.scalar.activation(penalty[:], neg_y[j][:], ACT.Relu, scale=0.4, bias=knee[:, j : j + 1])
            for cols in halves if j == PACK - 1 else [slice(0, V)]:
                nc.vector.scalar_tensor_tensor(
                    out=neg_util[:, j, cols],
                    in0=neg_y[j][:, cols],
                    scalar=base_sb[:, j : j + 1],
                    in1=penalty[:, cols],
                    op0=ALU.subtract,
                    op1=ALU.min,
                )

        wu_rows = sbuf("wu_rows", [P, PACK, V], BF16)
        for j in range(2):
            nc.scalar.activation(wu_rows[:, j, :], neg_util[:, j, :], ACT.Copy, scale=neg_isig[:, j : j + 1])
        for j, cols in ((2, slice(0, V)), (3, halves[0]), (3, halves[1])):
            nc.vector.tensor_scalar(
                out=wu_rows[:, j, cols],
                in0=neg_util[:, j, cols],
                scalar1=neg_isig[:, j : j + 1],
                scalar2=None,
                op0=ALU.mult,
            )
        wu = [sbuf("wu%d" % h, [P, HALF, PACK], BF16) for h in range(2)]
        for h, cols in enumerate(halves):
            nc.vector.tensor_copy(wu[h][:], wu_rows[:, :, cols].rearrange("p j v -> p v j"))

        grad = [psum.tile([P, HALF], F32, name="grad%d" % h) for h in range(2)]
        square_sum = [sbuf("square_sum%d" % h, [P, 1], F32) for h in range(2)]
        first_part = sbuf("first_part", [P, 1], F32)
        for h in range(2):
            wu_codes, wu_scales = quantize("wu%d" % h, wu[h][:], HALF)
            nc.tensor.matmul_mx(
                out=grad[h][:],
                lhsT=pert_codes[:].bitcast(FP8X4),
                lhsT_scale=pert_scales[:],
                rhs=wu_codes[:].bitcast(FP8X4),
                rhs_scale=wu_scales[:],
                start=True,
                stop=True,
            )
            squares = sbuf("squares%d" % h, [P, HALF], F32)
            nc.scalar.activation(squares[:], grad[h][:], ACT.Square, accum_out=square_sum[h][:])
            if h == 0:
                nc.scalar.activation(first_part[:], square_sum[0][:], ACT.Copy, scale=1.0 / V, bias=0.1)

        inv_rms = sbuf("inv_rms", [P, 1], F32)
        nc.scalar.activation(inv_rms[:], square_sum[1][:], ACT.Abs_reciprocal_sqrt, scale=1.0 / V, bias=first_part[:])
        for h, (cols, queue) in enumerate(zip(halves, (nc.sync, nc.scalar))):
            result = sbuf("result%d" % h, [P, HALF], F32)
            nc.vector.scalar_tensor_tensor(
                out=result[:], in0=grad[h][:], scalar=inv_rms[:], in1=theta_sb[:, cols], op0=ALU.mult, op1=ALU.add
            )
            queue.dma_start(out=out[:, cols], in_=result[:])
